import numpy as np
import ml_dtypes


def mxq(x, axis, fmt="e4m3"):
    dtype, down = {"e4m3": (ml_dtypes.float8_e4m3fn, 7), "e5m2": (ml_dtypes.float8_e5m2, 14)}[fmt]
    v = np.moveaxis(np.asarray(x, np.float32).astype(ml_dtypes.bfloat16).astype(np.float64), axis, -1)
    blocks = v.reshape(v.shape[:-1] + (-1, 32))
    amax = np.abs(blocks).max(-1, keepdims=True)
    byte = np.maximum(np.where(amax > 0, np.frexp(amax)[1] - 1 + 127, 0) - down, 1)
    scale = np.exp2(byte - 127.0)
    codes = (blocks / scale).astype(np.float32).astype(dtype).astype(np.float64)
    return np.moveaxis((codes * scale).reshape(v.shape), -1, axis)


WIDE = False


def mx_kscale(k):
    if not WIDE:
        return np.ones(k)
    levels = np.array([10, -10, 5, -5, 0])
    if k % 512:
        return np.exp2(np.random.permutation(np.resize(levels, k // 32))).repeat(32)
    a = np.empty((k // 512, 16))
    for p in range(k // 512):
        a[p, :8] = np.random.permutation(np.resize(levels, 8))
        for g in range(8):
            far = levels[np.abs(levels - a[p, g]) >= 10]
            a[p, g + 8] = far[np.random.randint(len(far))]
    return np.exp2(a.ravel()).repeat(32)


def f64(x):
    return np.asarray(x).astype(np.float64)


def striped(idx):
    return np.tile(np.asarray(idx).reshape(-1, 16).T, (8, 1)).astype(np.uint16)


def unstriped(offs):
    return offs[:16].T.reshape(-1).astype(np.int64)


E2M1 = np.array([0.0, 0.5, 1.0, 1.5, 2.0, 3.0, 4.0, 6.0, -0.0, -0.5, -1.0, -1.5, -2.0, -3.0, -4.0, -6.0])


def pack_weight(w, fmt):
    k, n = w.shape
    w = f64(np.asarray(w, np.float32).astype(ml_dtypes.bfloat16)).reshape(k // 32, 32, n)
    amax = np.abs(w).max(1)
    if fmt == "e4m3":
        byte = np.frexp(amax)[1] - 1 + 127 - 7
    else:
        mant, ex = np.frexp(amax / 6.0)
        byte = np.where(mant > 0.5, ex, ex - 1) + 127
    byte = np.clip(np.where(amax > 0, byte, 1), 1, 254)
    scaled = (w * np.exp2(127.0 - byte)[:, None, :]).reshape(k, n).astype(np.float32)
    by_word = np.ascontiguousarray(scaled.reshape(k // 512, 128, 4, n).transpose(0, 1, 3, 2))
    if fmt == "e4m3":
        words = by_word.astype(ml_dtypes.float8_e4m3fn).view(np.uint8)
    else:
        c = by_word.astype(ml_dtypes.float4_e2m1fn).view(np.uint8) & 0xF
        words = (c[..., 0::2] | (c[..., 1::2] << 4)).reshape(k // 512, 128, 2 * n)
    return np.ascontiguousarray(words), np.ascontiguousarray(byte.astype(np.uint8).reshape(k // 512, 16, n))


def unpack_weight(words, scales, fmt):
    g, _, n = scales.shape
    words = np.ascontiguousarray(words).reshape(g, 128, n, -1)
    if fmt == "e4m3":
        vals = words.view(ml_dtypes.float8_e4m3fn).astype(np.float64)
    else:
        nib = np.empty((g, 128, n, 4), np.uint8)
        nib[..., 0::2] = words & 0xF
        nib[..., 1::2] = words >> 4
        vals = E2M1[nib]
    vals = vals * np.repeat(np.exp2(scales.astype(np.float64) - 127.0), 8, axis=1)[..., None]
    return vals.transpose(0, 1, 3, 2).reshape(g * 512, n)


def bf(x):
    return np.asarray(x, np.float32).astype(ml_dtypes.bfloat16)


def planes(Y):
    r, m = Y.shape
    b = f64(bf(Y)).reshape(r // 32, 32, m)
    amax = np.abs(b).max(1)
    byte = np.clip(np.where(amax > 0, np.frexp(amax)[1] - 1 + 127 - 7, 1), 1, 254)
    codes = (b * np.exp2(127.0 - byte)[:, None, :]).reshape(r, m).astype(np.float32).astype(ml_dtypes.float8_e4m3fn).view(np.uint8)
    words = codes.reshape(r // 512, 128, 4, m).transpose(0, 1, 3, 2)
    return np.ascontiguousarray(words), np.ascontiguousarray(byte.astype(np.uint8).reshape(r // 512, 16, m))


K, S, T, N, L = 1024, 512, 512, 512, 512


def setup_inputs():
    n = np.random.standard_normal
    idx = np.random.randint(0, S, T)
    idx2 = np.random.randint(0, S, T)
    fk = mx_kscale(K)
    fl = mx_kscale(L)
    xbp = pack_weight(n((K, S)) / fk[:, None], "e2m1")
    wap = pack_weight(n((K, N)) * 1 / np.sqrt(K) * fk[:, None], "e4m3")
    wtp = pack_weight(n((L, N)) * 1 / np.sqrt(L) * fl[:, None], "e2m1")
    return {
        "xb_words": xbp[0],
        "xb_scales": xbp[1],
        "wa_words": wap[0],
        "wa_scales": wap[1],
        "ga": (np.random.uniform(0.4, 1.0, (1, T))).astype(np.float32),
        "gb": (np.random.uniform(0.1, 0.6, (1, T))).astype(np.float32),
        "xt": (n((L, T)) / fl[:, None]).astype(np.float32),
        "wt_words": wtp[0],
        "wt_scales": wtp[1],
        "offs": striped(idx),
        "offs2": striped(idx2),
    }


def reference(xb_words, xb_scales, wa_words, wa_scales, ga, gb, xt, wt_words, wt_scales, offs, offs2):
    idx = unstriped(offs)
    idx2 = unstriped(offs2)
    xbu = unpack_weight(xb_words, xb_scales, "e2m1")
    wau = unpack_weight(wa_words, wa_scales, "e4m3")
    wtu = unpack_weight(wt_words, wt_scales, "e2m1")
    z = wau.T @ xbu
    xtq = mxq(f64(xt), 0, "e4m3")
    q = wtu.T @ xtq
    y = f64(ga) * z[:, idx] + f64(gb) * z[:, idx2] + q
    words, scales = planes(y)
    return y, words, scales

@@ -1,0 +1,194 @@
+from contextlib import ExitStack
+
+import concourse.mybir as mybir
+from concourse.masks import make_identity
+
+K, S, T, N, L = 1024, 512, 512, 512, 512
+FLOPS = 2 * K * N * S + 2 * L * N * T
+
+F32 = mybir.dt.float32
+BF16 = mybir.dt.bfloat16
+I32 = mybir.dt.int32
+U32 = mybir.dt.uint32
+U16 = mybir.dt.uint16
+U8 = mybir.dt.uint8
+FP8X4 = mybir.dt.float8_e4m3fn_x4
+FP4X4 = mybir.dt.float4_e2m1fn_x4
+MULT = mybir.AluOpType.mult
+ADD = mybir.AluOpType.add
+
+P = 128
+PACK = 4
+PASSES = K // (P * PACK)
+BANK = 512
+CHUNKS = ((0, 256), (256, 128), (384, 128))
+
+
+def load_scale_rows(queue, plane, scales):
+    for quad in range(4):
+        queue.dma_start(
+            out=plane[32 * quad : 32 * quad + 4, :, :].bitcast(I32),
+            in_=scales[:, 4 * quad : 4 * quad + 4, :].rearrange("z r c -> r z c").bitcast(I32),
+        )
+
+
+def tile_moe_buffer_read_twice_pl_kernel(
+    tc, xb_words, xb_scales, wa_words, wa_scales, ga, gb, xt, wt_words, wt_scales, offs, offs2, out_0, out_1, out_2
+):
+    nc = tc.nc
+    with ExitStack() as ctx:
+        lists = ctx.enter_context(tc.tile_pool(name="lists", bufs=1))
+        keep = ctx.enter_context(tc.tile_pool(name="keep", bufs=1))
+        psum = ctx.enter_context(tc.psum_pool(name="psum", bufs=1))
+
+        def bank(b, shape):
+            return psum.tile(shape, F32, name="bank%d" % b, tag="bank%d" % b)
+
+        wa_plane_raw = keep.tile([P, PASSES, N], U8, name="wa_plane_raw", align_bytes=64)
+        xb_plane = keep.tile([P, PASSES, S], U8, name="xb_plane", align_bytes=64)
+        wt_plane_raw = keep.tile([P, 1, N], U8, name="wt_plane_raw", align_bytes=64)
+        for plane in (wa_plane_raw, xb_plane):
+            nc.vector.memset(plane[:].bitcast(I32), 0)
+        nc.gpsimd.memset(wt_plane_raw[:].bitcast(I32), 0)
+
+        load_scale_rows(nc.sync, wa_plane_raw, wa_scales)
+        wa_raw = [keep.tile([P, N], I32, name="wa_raw%d" % z) for z in range(PASSES)]
+        for z in range(PASSES):
+            nc.sync.dma_start(out=wa_raw[z][:], in_=wa_words[z].rearrange("p n r -> p (n r)").bitcast(I32))
+        xb_codes = keep.tile([P, PASSES, 2 * S], U8, name="xb_codes", align_bytes=64)
+        nc.sync.dma_start(out=xb_codes[:].bitcast(I32), in_=xb_words.rearrange("z p c -> p z c").bitcast(I32))
+        load_scale_rows(nc.sync, xb_plane, xb_scales)
+
+        gate_cols = [keep.tile([P, PACK], F32, name="gate_col%d" % i) for i in range(2)]
+        for col, gate in zip(gate_cols, (ga, gb)):
+            nc.sync.dma_start(out=col[:], in_=gate.rearrange("o (p c) -> (o p) c", c=PACK))
+        offsets = [lists.tile([P, T // 16], U16, name="offsets%d" % i) for i in range(2)]
+        nc.sync.dma_start(offsets[0][:], offs)
+        nc.sync.dma_start(offsets[1][:], offs2)
+
+        load_scale_rows(nc.gpsimd, wt_plane_raw, wt_scales)
+        xt_rows = xt.rearrange("(p j) t -> p j t", j=PACK)
+        xt_raw = [keep.tile([P, PACK, w], F32, name="xt_raw%d" % t0) for t0, w in CHUNKS]
+        nc.sync.dma_start(out=xt_raw[0][:], in_=xt_rows[:, :, CHUNKS[0][0] : CHUNKS[0][0] + CHUNKS[0][1]])
+        wt_raw = keep.tile([P, 2 * N], U8, name="wt_raw")
+        nc.sync.dma_start(out=wt_raw[:].bitcast(I32), in_=wt_words[0].bitcast(I32))
+        for c in range(1, len(CHUNKS)):
+            t0, w = CHUNKS[c]
+            nc.sync.dma_start(out=xt_raw[c][:], in_=xt_rows[:, :, t0 : t0 + w])
+
+        ident = keep.tile([P, P], F32, name="ident")
+        make_identity(nc, ident[:])
+
+        wa_plane = keep.tile([P, PASSES, N], U8, name="wa_plane", align_bytes=64)
+        nc.vector.tensor_copy(
+            out=wa_plane[:].rearrange("p z (j m) -> p z m j", j=PACK),
+            in_=wa_plane_raw[:].rearrange("p z (m j) -> p z m j", j=PACK),
+        )
+        wa_codes = [keep.tile([P, N], U32, name="wa_codes%d" % z, align_bytes=64) for z in range(PASSES)]
+        for z in range(PASSES):
+            nc.vector.tensor_copy(
+                out=wa_codes[z][:].bitcast(I32).rearrange("p (j m) -> p m j", j=PACK),
+                in_=wa_raw[z][:].rearrange("p (m j) -> p m j", j=PACK),
+            )
+
+        gates = []
+        for i in range(2):
+            spread = bank(6 + i, [P, PACK, P])
+            for c in range(PACK):
+                nc.tensor.transpose(spread[:, c, :], gate_cols[i][:, c : c + 1].to_broadcast([P, P]), ident[:])
+            row = keep.tile([P, T], F32, name="gate_row%d" % i)
+            nc.scalar.copy(out=row[:].rearrange("p (m c) -> p m c", c=PACK), in_=spread[:].rearrange("p c m -> p m c"))
+            gates.append(row)
+
+        z_rows = []
+        for j in range(PACK):
+            acc = bank(j, [P, S])
+            for z in range(PASSES):
+                nc.tensor.matmul_mx(
+                    out=acc[:],
+                    lhsT=wa_codes[z][:, j * P : (j + 1) * P].bitcast(FP8X4),
+                    lhsT_scale=wa_plane[:, z, j * P : (j + 1) * P],
+                    rhs=xb_codes[:, z, :].bitcast(FP4X4),
+                    rhs_scale=xb_plane[:, z, :],
+                    start=(z == 0),
+                    stop=(z == PASSES - 1),
+                )
+            z_row = keep.tile([P, S], F32, name="z_row%d" % j)
+            nc.scalar.copy(out=z_row[:], in_=acc[:])
+            z_rows.append(z_row)
+
+        wt_plane = keep.tile([P, N], U8, name="wt_plane", align_bytes=64)
+        nc.vector.tensor_copy(
+            out=wt_plane[:].rearrange("p (j m) -> p m j", j=PACK),
+            in_=wt_plane_raw[:, 0, :].rearrange("p (m j) -> p m j", j=PACK),
+        )
+        wt_codes = keep.tile([P, 2 * N], U8, name="wt_codes", align_bytes=64)
+        nc.vector.tensor_copy(
+            out=wt_codes[:].bitcast(U16).rearrange("p (j m) -> p m j", j=PACK),
+            in_=wt_raw[:].bitcast(U16).rearrange("p (m j) -> p m j", j=PACK),
+        )
+
+        def interleave(dst, src):
+            nc.scalar.copy(
+                out=dst[:].rearrange("p (c i) j -> p c j i", i=4),
+                in_=src[:].rearrange("p j (c i) -> p c j i", i=4),
+            )
+
+        q_banks = []
+        next_bank = 4
+        for c, (t0, w) in enumerate(CHUNKS):
+            xt_bf = keep.tile([P, w, PACK], BF16, name="xt_bf%d" % c, align_bytes=64)
+            interleave(xt_bf, xt_raw[c])
+            xt_codes = keep.tile([P, w], U32, name="xt_codes%d" % c, align_bytes=64)
+            xt_plane = keep.tile([P, w], U8, name="xt_plane%d" % c, align_bytes=64)
+            nc.vector.quantize_mx(
+                out=xt_codes[:].bitcast(FP8X4), scales=xt_plane[:], in_=xt_bf[:].rearrange("p t j -> p (t j)")
+            )
+            per_bank = BANK // w
+            held = []
+            for j0 in range(0, PACK, per_bank):
+                acc = bank(next_bank, [P, per_bank, w])
+                next_bank = next_bank + 1
+                for j in range(j0, j0 + per_bank):
+                    nc.tensor.matmul_mx(
+                        out=acc[:, j - j0, :],
+                        lhsT=wt_codes[:, 2 * j * P : 2 * (j + 1) * P].bitcast(FP4X4),
+                        lhsT_scale=wt_plane[:, j * P : (j + 1) * P],
+                        rhs=xt_codes[:].bitcast(FP8X4),
+                        rhs_scale=xt_plane[:],
+                        start=True,
+                        stop=True,
+                    )
+                held.append((j0, per_bank, acc))
+            q_banks.append(held)
+
+        out_rows = out_0.rearrange("(p j) t -> p j t", j=PACK)
+        out_words = out_1[0].rearrange("p t r -> p (t r)").bitcast(I32)
+        y_plane = keep.tile([P, T], U8, name="y_plane", align_bytes=64)
+        for c, (t0, w) in enumerate(CHUNKS):
+            cols = slice(t0 // 16, (t0 + w) // 16)
+            picked = [keep.tile([P, PACK, w], F32, name="picked%d_%d" % (i, c)) for i in range(2)]
+            for j in range(PACK):
+                for i in range(2):
+                    nc.vector.tensor_tensor(
+                        picked[i][:, j, :], z_rows[j][:].indirect(offsets[i][:, cols]), gates[i][:, t0 : t0 + w], MULT
+                    )
+            part = keep.tile([P, PACK, w], F32, name="part%d" % c)
+            for j0, count, acc in q_banks[c]:
+                nc.vector.tensor_tensor(part[:, j0 : j0 + count, :], picked[0][:, j0 : j0 + count, :], acc[:], ADD)
+            y = keep.tile([P, PACK, w], F32, name="y%d" % c)
+            nc.vector.tensor_tensor(y[:], part[:], picked[1][:], ADD)
+            nc.sync.dma_start(out=out_rows[:, :, t0 : t0 + w], in_=y[:])
+            y_bf = keep.tile([P, w, PACK], BF16, name="y_bf%d" % c, align_bytes=64)
+            interleave(y_bf, y)
+            y_codes = keep.tile([P, w], U32, name="y_codes%d" % c, align_bytes=64)
+            nc.vector.quantize_mx(
+                out=y_codes[:].bitcast(FP8X4), scales=y_plane[:, t0 : t0 + w], in_=y_bf[:].rearrange("p t j -> p (t j)")
+            )
+            nc.sync.dma_start(out=out_words[:, t0 : t0 + w], in_=y_codes[:].bitcast(I32))
+        for quad in range(4):
+            queue = nc.sync if quad % 2 == 0 else nc.scalar
+            queue.dma_start(
+                out=out_2[0, 4 * quad : 4 * quad + 4, :].bitcast(I32),
+                in_=y_plane[32 * quad : 32 * quad + 4, :].bitcast(I32),
+            )

@@ -20,8 +20,9 @@ ADD = mybir.AluOpType.add
 P = 128
 PACK = 4
 PASSES = K // (P * PACK)
-BANK = 512
-CHUNKS = ((0, 256), (256, 128), (384, 128))
+HALF = T // 2
+BLOCKS = T // P
+STRETCHES = ((0, HALF), (HALF, P), (HALF + P, P))
 
 
 def load_scale_rows(queue, plane, scales):
@@ -41,43 +42,37 @@ def tile_moe_buffer_read_twice_pl_kernel(
         keep = ctx.enter_context(tc.tile_pool(name="keep", bufs=1))
         psum = ctx.enter_context(tc.psum_pool(name="psum", bufs=1))
 
-        def bank(b, shape):
-            return psum.tile(shape, F32, name="bank%d" % b, tag="bank%d" % b)
+        def bank(b):
+            return psum.tile([P, PACK, P], F32, name="bank%d" % b, tag="bank%d" % b)
 
         wa_plane_raw = keep.tile([P, PASSES, N], U8, name="wa_plane_raw", align_bytes=64)
         xb_plane = keep.tile([P, PASSES, S], U8, name="xb_plane", align_bytes=64)
-        wt_plane_raw = keep.tile([P, 1, N], U8, name="wt_plane_raw", align_bytes=64)
-        for plane in (wa_plane_raw, xb_plane):
+        wt_plane = keep.tile([P, 1, N], U8, name="wt_plane", align_bytes=64)
+        nc.gpsimd.memset(wa_plane_raw[:].bitcast(I32), 0)
+        ident = keep.tile([P, P], F32, name="ident")
+        make_identity(nc, ident[:])
+        for plane in (xb_plane, wt_plane):
             nc.vector.memset(plane[:].bitcast(I32), 0)
-        nc.gpsimd.memset(wt_plane_raw[:].bitcast(I32), 0)
 
         load_scale_rows(nc.sync, wa_plane_raw, wa_scales)
-        wa_raw = [keep.tile([P, N], I32, name="wa_raw%d" % z) for z in range(PASSES)]
-        for z in range(PASSES):
-            nc.sync.dma_start(out=wa_raw[z][:], in_=wa_words[z].rearrange("p n r -> p (n r)").bitcast(I32))
-        xb_codes = keep.tile([P, PASSES, 2 * S], U8, name="xb_codes", align_bytes=64)
-        nc.sync.dma_start(out=xb_codes[:].bitcast(I32), in_=xb_words.rearrange("z p c -> p z c").bitcast(I32))
-        load_scale_rows(nc.sync, xb_plane, xb_scales)
-
         gate_cols = [keep.tile([P, PACK], F32, name="gate_col%d" % i) for i in range(2)]
         for col, gate in zip(gate_cols, (ga, gb)):
             nc.sync.dma_start(out=col[:], in_=gate.rearrange("o (p c) -> (o p) c", c=PACK))
+        wa_raw = keep.tile([P, PASSES, N], I32, name="wa_raw")
+        nc.sync.dma_start(out=wa_raw[:], in_=wa_words.rearrange("z p n r -> p z (n r)").bitcast(I32))
+        xb_codes = keep.tile([P, PASSES, 2 * S], U8, name="xb_codes", tag="relay", align_bytes=64)
+        nc.sync.dma_start(out=xb_codes[:].bitcast(I32), in_=xb_words.rearrange("z p c -> p z c").bitcast(I32))
+        load_scale_rows(nc.sync, xb_plane, xb_scales)
         offsets = [lists.tile([P, T // 16], U16, name="offsets%d" % i) for i in range(2)]
         nc.sync.dma_start(offsets[0][:], offs)
         nc.sync.dma_start(offsets[1][:], offs2)
-
-        load_scale_rows(nc.gpsimd, wt_plane_raw, wt_scales)
         xt_rows = xt.rearrange("(p j) t -> p j t", j=PACK)
-        xt_raw = [keep.tile([P, PACK, w], F32, name="xt_raw%d" % t0) for t0, w in CHUNKS]
-        nc.sync.dma_start(out=xt_raw[0][:], in_=xt_rows[:, :, CHUNKS[0][0] : CHUNKS[0][0] + CHUNKS[0][1]])
-        wt_raw = keep.tile([P, 2 * N], U8, name="wt_raw")
-        nc.sync.dma_start(out=wt_raw[:].bitcast(I32), in_=wt_words[0].bitcast(I32))
-        for c in range(1, len(CHUNKS)):
-            t0, w = CHUNKS[c]
-            nc.sync.dma_start(out=xt_raw[c][:], in_=xt_rows[:, :, t0 : t0 + w])
-
-        ident = keep.tile([P, P], F32, name="ident")
-        make_identity(nc, ident[:])
+        xt_raw = [keep.tile([P, PACK, HALF], F32, name="xt_raw%d" % h, tag="xt_raw%d" % h) for h in range(2)]
+        nc.sync.dma_start(out=xt_raw[0][:], in_=xt_rows[:, :, :HALF])
+        wt_codes = keep.tile([P, 2 * N], U8, name="wt_codes", align_bytes=64)
+        nc.sync.dma_start(out=wt_codes[:].bitcast(I32), in_=wt_words[0].bitcast(I32))
+        load_scale_rows(nc.sync, wt_plane, wt_scales)
+        nc.sync.dma_start(out=xt_raw[1][:], in_=xt_rows[:, :, HALF:])
 
         wa_plane = keep.tile([P, PASSES, N], U8, name="wa_plane", align_bytes=64)
         nc.vector.tensor_copy(
@@ -88,24 +83,30 @@ def tile_moe_buffer_read_twice_pl_kernel(
         for z in range(PASSES):
             nc.vector.tensor_copy(
                 out=wa_codes[z][:].bitcast(I32).rearrange("p (j m) -> p m j", j=PACK),
-                in_=wa_raw[z][:].rearrange("p (m j) -> p m j", j=PACK),
+                in_=wa_raw[:, z, :].rearrange("p (m j) -> p m j", j=PACK),
             )
 
         gates = []
         for i in range(2):
-            spread = bank(6 + i, [P, PACK, P])
+            spread = bank(4 + i)
             for c in range(PACK):
                 nc.tensor.transpose(spread[:, c, :], gate_cols[i][:, c : c + 1].to_broadcast([P, P]), ident[:])
-            row = keep.tile([P, T], F32, name="gate_row%d" % i)
-            nc.scalar.copy(out=row[:].rearrange("p (m c) -> p m c", c=PACK), in_=spread[:].rearrange("p c m -> p m c"))
-            gates.append(row)
+            rows = []
+            for s, (t0, w) in enumerate(STRETCHES):
+                row = keep.tile([P, w], F32, name="gate%d_%d" % (i, s), tag="gate%d_%d" % (i, s), align_bytes=64)
+                nc.scalar.copy(
+                    out=row[:].rearrange("p (m c) -> p m c", c=PACK),
+                    in_=spread[:, :, t0 // PACK : (t0 + w) // PACK].rearrange("p c m -> p m c"),
+                )
+                rows.append(row)
+            gates.append(rows)
 
         z_rows = []
         for j in range(PACK):
-            acc = bank(j, [P, S])
+            acc = bank(j)
             for z in range(PASSES):
                 nc.tensor.matmul_mx(
-                    out=acc[:],
+                    out=acc[:].rearrange("p a b -> p (a b)"),
                     lhsT=wa_codes[z][:, j * P : (j + 1) * P].bitcast(FP8X4),
                     lhsT_scale=wa_plane[:, z, j * P : (j + 1) * P],
                     rhs=xb_codes[:, z, :].bitcast(FP4X4),
@@ -114,78 +115,130 @@ def tile_moe_buffer_read_twice_pl_kernel(
                     stop=(z == PASSES - 1),
                 )
             z_row = keep.tile([P, S], F32, name="z_row%d" % j)
-            nc.scalar.copy(out=z_row[:], in_=acc[:])
+            nc.scalar.copy(out=z_row[:], in_=acc[:].rearrange("p a b -> p (a b)"))
             z_rows.append(z_row)
 
-        wt_plane = keep.tile([P, N], U8, name="wt_plane", align_bytes=64)
-        nc.vector.tensor_copy(
-            out=wt_plane[:].rearrange("p (j m) -> p m j", j=PACK),
-            in_=wt_plane_raw[:, 0, :].rearrange("p (m j) -> p m j", j=PACK),
-        )
-        wt_codes = keep.tile([P, 2 * N], U8, name="wt_codes", align_bytes=64)
-        nc.vector.tensor_copy(
-            out=wt_codes[:].bitcast(U16).rearrange("p (j m) -> p m j", j=PACK),
-            in_=wt_raw[:].bitcast(U16).rearrange("p (m j) -> p m j", j=PACK),
-        )
+        def interleave(copy, dst, src):
+            copy(out=dst.rearrange("p (c i) j -> p c j i", i=4), in_=src.rearrange("p j (c i) -> p c j i", i=4))
 
-        def interleave(dst, src):
-            nc.scalar.copy(
-                out=dst[:].rearrange("p (c i) j -> p c j i", i=4),
-                in_=src[:].rearrange("p j (c i) -> p c j i", i=4),
-            )
-
-        q_banks = []
-        next_bank = 4
-        for c, (t0, w) in enumerate(CHUNKS):
-            xt_bf = keep.tile([P, w, PACK], BF16, name="xt_bf%d" % c, align_bytes=64)
-            interleave(xt_bf, xt_raw[c])
-            xt_codes = keep.tile([P, w], U32, name="xt_codes%d" % c, align_bytes=64)
-            xt_plane = keep.tile([P, w], U8, name="xt_plane%d" % c, align_bytes=64)
+        xt_codes = keep.tile([P, T], U32, name="xt_codes", align_bytes=64)
+        xt_plane = keep.tile([P, T], U8, name="xt_plane", align_bytes=64)
+        for h in range(2):
+            xt_bf = keep.tile([P, HALF, PACK], BF16, name="xt_bf%d" % h, tag=("lead", "relay")[h], align_bytes=64)
+            for b in range(2):
+                interleave(nc.scalar.copy, xt_bf[:, b * P : (b + 1) * P, :], xt_raw[h][:, :, b * P : (b + 1) * P])
             nc.vector.quantize_mx(
-                out=xt_codes[:].bitcast(FP8X4), scales=xt_plane[:], in_=xt_bf[:].rearrange("p t j -> p (t j)")
+                out=xt_codes[:, h * HALF : (h + 1) * HALF].bitcast(FP8X4),
+                scales=xt_plane[:, h * HALF : (h + 1) * HALF],
+                in_=xt_bf[:].rearrange("p t j -> p (t j)"),
             )
-            per_bank = BANK // w
-            held = []
-            for j0 in range(0, PACK, per_bank):
-                acc = bank(next_bank, [P, per_bank, w])
-                next_bank = next_bank + 1
-                for j in range(j0, j0 + per_bank):
-                    nc.tensor.matmul_mx(
-                        out=acc[:, j - j0, :],
-                        lhsT=wt_codes[:, 2 * j * P : 2 * (j + 1) * P].bitcast(FP4X4),
-                        lhsT_scale=wt_plane[:, j * P : (j + 1) * P],
-                        rhs=xt_codes[:].bitcast(FP8X4),
-                        rhs_scale=xt_plane[:],
-                        start=True,
-                        stop=True,
-                    )
-                held.append((j0, per_bank, acc))
-            q_banks.append(held)
+
+        q_turned = []
+        for b in range(BLOCKS):
+            acc = bank((6, 7, 4, 5)[b])
+            flat = acc[:].rearrange("p a b -> p (a b)")
+            nc.tensor.matmul_mx(
+                out=flat,
+                lhsT=xt_codes[:, b * P : (b + 1) * P].bitcast(FP8X4),
+                lhsT_scale=xt_plane[:, b * P : (b + 1) * P],
+                rhs=wt_codes[:].bitcast(FP4X4),
+                rhs_scale=wt_plane[:, 0, :],
+                start=True,
+                stop=True,
+            )
+            held = keep.tile([P, PACK, P], F32, name="q_turned%d" % b)
+            nc.scalar.copy(out=held[:], in_=flat.rearrange("p (m j) -> p j m", j=PACK))
+            q_turned.append(held)
+
+        first = keep.tile([P, PACK - 1, 2, HALF], F32, name="first")
+        first_end = keep.tile([P, 2, HALF], F32, name="first_end", tag="lead", align_bytes=64)
+        second = keep.tile([P, PACK, 2, P], F32, name="second", tag="relay", align_bytes=64)
+        third = keep.tile([P, 2, PACK, P], F32, name="third", tag="gate0_1", align_bytes=64)
+
+        def picked(s, i, j):
+            if s == 0:
+                return first[:, j, i, :] if j < PACK - 1 else first_end[:, i, :]
+            return second[:, j, i, :] if s == 1 else third[:, i, j, :]
+
+        def look_up(s, i, j):
+            t0, w = STRETCHES[s]
+            nc.vector.tensor_tensor(
+                picked(s, i, j), z_rows[j][:].indirect(offsets[i][:, t0 // 16 : (t0 + w) // 16]), gates[i][s][:], MULT
+            )
 
         out_rows = out_0.rearrange("(p j) t -> p j t", j=PACK)
         out_words = out_1[0].rearrange("p t r -> p (t r)").bitcast(I32)
         y_plane = keep.tile([P, T], U8, name="y_plane", align_bytes=64)
-        for c, (t0, w) in enumerate(CHUNKS):
-            cols = slice(t0 // 16, (t0 + w) // 16)
-            picked = [keep.tile([P, PACK, w], F32, name="picked%d_%d" % (i, c)) for i in range(2)]
+
+        def add_pair(b):
+            s, c0 = (0, b * P) if b < 2 else (1, 0)
+            pair = bank((0, 1, 2)[b])
             for j in range(PACK):
                 for i in range(2):
-                    nc.vector.tensor_tensor(
-                        picked[i][:, j, :], z_rows[j][:].indirect(offsets[i][:, cols]), gates[i][:, t0 : t0 + w], MULT
+                    nc.tensor.matmul(
+                        pair[:, j, :], picked(s, i, j)[:, c0 : c0 + P], ident[:],
+                        start=(i == 0), stop=(i == 1), is_transpose=True,
                     )
-            part = keep.tile([P, PACK, w], F32, name="part%d" % c)
-            for j0, count, acc in q_banks[c]:
-                nc.vector.tensor_tensor(part[:, j0 : j0 + count, :], picked[0][:, j0 : j0 + count, :], acc[:], ADD)
-            y = keep.tile([P, PACK, w], F32, name="y%d" % c)
-            nc.vector.tensor_tensor(y[:], part[:], picked[1][:], ADD)
-            nc.sync.dma_start(out=out_rows[:, :, t0 : t0 + w], in_=y[:])
-            y_bf = keep.tile([P, w, PACK], BF16, name="y_bf%d" % c, align_bytes=64)
-            interleave(y_bf, y)
-            y_codes = keep.tile([P, w], U32, name="y_codes%d" % c, align_bytes=64)
+            pair_turned = keep.tile(
+                [P, PACK, P], F32, name="pair_turned%d" % b, tag=("xt_raw1", "pair1", "pair2")[b]
+            )
+            nc.scalar.copy(out=pair_turned[:], in_=pair[:])
+            return pair_turned
+
+        def add_q(b, pair_turned):
+            total = bank((2, 3, 6)[b])
+            for j in range(PACK):
+                for i, term in enumerate((q_turned[b], pair_turned)):
+                    nc.tensor.matmul(
+                        total[:, j, :], term[:, j, :], ident[:], start=(i == 0), stop=(i == 1), is_transpose=True
+                    )
+            y = keep.tile([P, PACK, P], F32, name="y%d" % b)
+            nc.scalar.copy(out=y[:], in_=total[:])
+            nc.sync.dma_start(out=out_rows[:, :, b * P : (b + 1) * P], in_=y[:])
+            return y
+
+        def quantise(t0, w, y_bf, tag):
+            y_codes = keep.tile([P, w], U32, name="y_codes%d" % t0, tag=tag, align_bytes=64)
             nc.vector.quantize_mx(
                 out=y_codes[:].bitcast(FP8X4), scales=y_plane[:, t0 : t0 + w], in_=y_bf[:].rearrange("p t j -> p (t j)")
             )
             nc.sync.dma_start(out=out_words[:, t0 : t0 + w], in_=y_codes[:].bitcast(I32))
+
+        for j in range(PACK):
+            for i in range(2):
+                look_up(0, i, j)
+        pairs = [add_pair(b) for b in range(2)]
+        ys = [add_q(b, pairs[b]) for b in range(2)]
+        for j in range(PACK):
+            for i in range(2):
+                look_up(1, i, j)
+        pair2 = add_pair(2)
+        q_last = bank(7)
+        for j in range(PACK):
+            nc.tensor.transpose(q_last[:, j, :], q_turned[BLOCKS - 1][:, j, :], ident[:])
+        y_bf_first = keep.tile([P, HALF, PACK], BF16, name="y_bf_first", tag="relay", align_bytes=64)
+        for b in range(2):
+            interleave(nc.scalar.copy, y_bf_first[:, b * P : (b + 1) * P, :], ys[b][:])
+        y2 = add_q(2, pair2)
+        y_bf2 = keep.tile([P, P, PACK], BF16, name="y_bf2", align_bytes=64)
+        interleave(nc.scalar.copy, y_bf2[:], y2[:])
+
+        for j in range(PACK):
+            look_up(2, 0, j)
+        look_up(2, 1, 0)
+        part = keep.tile([P, PACK, P], F32, name="part", tag="part", align_bytes=64)
+        nc.vector.tensor_tensor(part[:], third[:, 0, :, :], q_last[:], ADD)
+        for j in range(1, PACK):
+            look_up(2, 1, j)
+        y3 = keep.tile([P, PACK, P], F32, name="y3")
+        nc.vector.tensor_tensor(y3[:], part[:], third[:, 1, :, :], ADD)
+        nc.sync.dma_start(out=out_rows[:, :, T - P :], in_=y3[:])
+        y_bf3 = keep.tile([P, P, PACK], BF16, name="y_bf3", align_bytes=64)
+        interleave(nc.vector.tensor_copy, y_bf3[:], y3[:])
+        quantise(0, HALF, y_bf_first, "part")
+        quantise(T - P, P, y_bf3, "codes3")
+        quantise(HALF, P, y_bf2, "gate0_1")
+
         for quad in range(4):
             queue = nc.sync if quad % 2 == 0 else nc.scalar
             queue.dma_start(

@@ -22,7 +22,7 @@ PACK = 4
 PASSES = K // (P * PACK)
 HALF = T // 2
 BLOCKS = T // P
-STRETCHES = ((0, HALF), (HALF, P), (HALF + P, P))
+STRETCHES = ((0, HALF), (HALF, HALF))
 
 
 def load_scale_rows(queue, plane, scales):
@@ -45,22 +45,23 @@ def tile_moe_buffer_read_twice_pl_kernel(
         def bank(b):
             return psum.tile([P, PACK, P], F32, name="bank%d" % b, tag="bank%d" % b)
 
+        wa_rows = keep.tile([P, PASSES, N], U8, name="wa_rows", align_bytes=64)
         wa_plane_raw = keep.tile([P, PASSES, N], U8, name="wa_plane_raw", align_bytes=64)
         xb_plane = keep.tile([P, PASSES, S], U8, name="xb_plane", align_bytes=64)
         wt_plane = keep.tile([P, 1, N], U8, name="wt_plane", align_bytes=64)
-        nc.gpsimd.memset(wa_plane_raw[:].bitcast(I32), 0)
+        nc.gpsimd.memset(xb_plane[:].bitcast(I32), 0)
         ident = keep.tile([P, P], F32, name="ident")
         make_identity(nc, ident[:])
-        for plane in (xb_plane, wt_plane):
+        for plane in (wt_plane, wa_plane_raw):
             nc.vector.memset(plane[:].bitcast(I32), 0)
 
-        load_scale_rows(nc.sync, wa_plane_raw, wa_scales)
+        load_scale_rows(nc.sync, wa_rows, wa_scales)
         gate_cols = [keep.tile([P, PACK], F32, name="gate_col%d" % i) for i in range(2)]
         for col, gate in zip(gate_cols, (ga, gb)):
             nc.sync.dma_start(out=col[:], in_=gate.rearrange("o (p c) -> (o p) c", c=PACK))
         wa_raw = keep.tile([P, PASSES, N], I32, name="wa_raw")
         nc.sync.dma_start(out=wa_raw[:], in_=wa_words.rearrange("z p n r -> p z (n r)").bitcast(I32))
-        xb_codes = keep.tile([P, PASSES, 2 * S], U8, name="xb_codes", tag="relay", align_bytes=64)
+        xb_codes = keep.tile([P, PASSES, 2 * S], U8, name="xb_codes", align_bytes=64)
         nc.sync.dma_start(out=xb_codes[:].bitcast(I32), in_=xb_words.rearrange("z p c -> p z c").bitcast(I32))
         load_scale_rows(nc.sync, xb_plane, xb_scales)
         offsets = [lists.tile([P, T // 16], U16, name="offsets%d" % i) for i in range(2)]
@@ -68,22 +69,25 @@ def tile_moe_buffer_read_twice_pl_kernel(
         nc.sync.dma_start(offsets[1][:], offs2)
         xt_rows = xt.rearrange("(p j) t -> p j t", j=PACK)
         xt_raw = [keep.tile([P, PACK, HALF], F32, name="xt_raw%d" % h, tag="xt_raw%d" % h) for h in range(2)]
-        nc.sync.dma_start(out=xt_raw[0][:], in_=xt_rows[:, :, :HALF])
+        nc.sync.dma_start(out=xt_raw[1][:], in_=xt_rows[:, :, HALF:])
         wt_codes = keep.tile([P, 2 * N], U8, name="wt_codes", align_bytes=64)
         nc.sync.dma_start(out=wt_codes[:].bitcast(I32), in_=wt_words[0].bitcast(I32))
         load_scale_rows(nc.sync, wt_plane, wt_scales)
-        nc.sync.dma_start(out=xt_raw[1][:], in_=xt_rows[:, :, HALF:])
+        nc.sync.dma_start(out=xt_raw[0][:], in_=xt_rows[:, :, :HALF])
 
-        wa_plane = keep.tile([P, PASSES, N], U8, name="wa_plane", align_bytes=64)
-        nc.vector.tensor_copy(
-            out=wa_plane[:].rearrange("p z (j m) -> p z m j", j=PACK),
-            in_=wa_plane_raw[:].rearrange("p z (m j) -> p z m j", j=PACK),
-        )
+        for quad in range(4):
+            rows = slice(32 * quad, 32 * quad + 4)
+            nc.vector.tensor_copy(out=wa_plane_raw[rows, :, :].bitcast(I32), in_=wa_rows[rows, :, :].bitcast(I32))
+        wa_planes = []
+        for j in range(PACK):
+            plane = keep.tile([P, PASSES, P], U8, name="wa_plane%d" % j, tag="chain%d" % j, align_bytes=64)
+            nc.vector.tensor_copy(out=plane[:], in_=wa_plane_raw[:].rearrange("p z (m j) -> p j z m", j=PACK)[:, j])
+            wa_planes.append(plane)
         wa_codes = [keep.tile([P, N], U32, name="wa_codes%d" % z, align_bytes=64) for z in range(PASSES)]
         for z in range(PASSES):
             nc.vector.tensor_copy(
-                out=wa_codes[z][:].bitcast(I32).rearrange("p (j m) -> p m j", j=PACK),
-                in_=wa_raw[:, z, :].rearrange("p (m j) -> p m j", j=PACK),
+                out=wa_codes[z][:].bitcast(I32).rearrange("p (j g i) -> p g j i", j=PACK, i=4),
+                in_=wa_raw[:, z, :].rearrange("p (g i j) -> p g j i", j=PACK, i=4),
             )
 
         gates = []
@@ -108,87 +112,83 @@ def tile_moe_buffer_read_twice_pl_kernel(
                 nc.tensor.matmul_mx(
                     out=acc[:].rearrange("p a b -> p (a b)"),
                     lhsT=wa_codes[z][:, j * P : (j + 1) * P].bitcast(FP8X4),
-                    lhsT_scale=wa_plane[:, z, j * P : (j + 1) * P],
+                    lhsT_scale=wa_planes[j][:, z, :],
                     rhs=xb_codes[:, z, :].bitcast(FP4X4),
                     rhs_scale=xb_plane[:, z, :],
                     start=(z == 0),
                     stop=(z == PASSES - 1),
                 )
-            z_row = keep.tile([P, S], F32, name="z_row%d" % j)
+            z_row = keep.tile([P, S], F32, name="z_row%d" % j, tag="z_row%d" % j, align_bytes=64)
             nc.scalar.copy(out=z_row[:], in_=acc[:].rearrange("p a b -> p (a b)"))
             z_rows.append(z_row)
 
         def interleave(copy, dst, src):
             copy(out=dst.rearrange("p (c i) j -> p c j i", i=4), in_=src.rearrange("p j (c i) -> p c j i", i=4))
 
-        xt_codes = keep.tile([P, T], U32, name="xt_codes", align_bytes=64)
+        xt_bf = {}
+        for j, b in enumerate((2, 3, 0, 1)):
+            xt_bf[b] = keep.tile([P, P, PACK], BF16, name="xt_bf%d" % b, tag="chain%d" % j, align_bytes=64)
+            interleave(nc.scalar.copy, xt_bf[b][:], xt_raw[b // 2][:, :, (b % 2) * P : (b % 2 + 1) * P])
         xt_plane = keep.tile([P, T], U8, name="xt_plane", align_bytes=64)
-        for h in range(2):
-            xt_bf = keep.tile([P, HALF, PACK], BF16, name="xt_bf%d" % h, tag=("lead", "relay")[h], align_bytes=64)
-            for b in range(2):
-                interleave(nc.scalar.copy, xt_bf[:, b * P : (b + 1) * P, :], xt_raw[h][:, :, b * P : (b + 1) * P])
+        xt_codes = {}
+
+        def quantise_xt(b, tag):
+            xt_codes[b] = keep.tile([P, P], U32, name="xt_codes%d" % b, tag=tag, align_bytes=64)
             nc.vector.quantize_mx(
-                out=xt_codes[:, h * HALF : (h + 1) * HALF].bitcast(FP8X4),
-                scales=xt_plane[:, h * HALF : (h + 1) * HALF],
-                in_=xt_bf[:].rearrange("p t j -> p (t j)"),
+                out=xt_codes[b][:].bitcast(FP8X4),
+                scales=xt_plane[:, b * P : (b + 1) * P],
+                in_=xt_bf[b][:].rearrange("p t j -> p (t j)"),
             )
 
-        q_turned = []
-        for b in range(BLOCKS):
-            acc = bank((6, 7, 4, 5)[b])
-            flat = acc[:].rearrange("p a b -> p (a b)")
+        def q_turned(b):
+            flat = bank((2, 3, 6, 7)[b])[:].rearrange("p a b -> p (a b)")
             nc.tensor.matmul_mx(
                 out=flat,
-                lhsT=xt_codes[:, b * P : (b + 1) * P].bitcast(FP8X4),
+                lhsT=xt_codes[b][:].bitcast(FP8X4),
                 lhsT_scale=xt_plane[:, b * P : (b + 1) * P],
                 rhs=wt_codes[:].bitcast(FP4X4),
                 rhs_scale=wt_plane[:, 0, :],
                 start=True,
                 stop=True,
             )
-            held = keep.tile([P, PACK, P], F32, name="q_turned%d" % b)
-            nc.scalar.copy(out=held[:], in_=flat.rearrange("p (m j) -> p j m", j=PACK))
-            q_turned.append(held)
+            nc.scalar.copy(out=q_held[:, b], in_=flat.rearrange("p (m j) -> p j m", j=PACK))
 
-        first = keep.tile([P, PACK - 1, 2, HALF], F32, name="first")
-        first_end = keep.tile([P, 2, HALF], F32, name="first_end", tag="lead", align_bytes=64)
-        second = keep.tile([P, PACK, 2, P], F32, name="second", tag="relay", align_bytes=64)
-        third = keep.tile([P, 2, PACK, P], F32, name="third", tag="gate0_1", align_bytes=64)
+        first = {}
 
-        def picked(s, i, j):
-            if s == 0:
-                return first[:, j, i, :] if j < PACK - 1 else first_end[:, i, :]
-            return second[:, j, i, :] if s == 1 else third[:, i, j, :]
-
-        def look_up(s, i, j):
+        def look_up(s, i, j, dst):
             t0, w = STRETCHES[s]
             nc.vector.tensor_tensor(
-                picked(s, i, j), z_rows[j][:].indirect(offsets[i][:, t0 // 16 : (t0 + w) // 16]), gates[i][s][:], MULT
+                dst, z_rows[j][:].indirect(offsets[i][:, t0 // 16 : (t0 + w) // 16]), gates[i][s][:], MULT
             )
 
         out_rows = out_0.rearrange("(p j) t -> p j t", j=PACK)
         out_words = out_1[0].rearrange("p t r -> p (t r)").bitcast(I32)
         y_plane = keep.tile([P, T], U8, name="y_plane", align_bytes=64)
 
-        def add_pair(b):
-            s, c0 = (0, b * P) if b < 2 else (1, 0)
-            pair = bank((0, 1, 2)[b])
-            for j in range(PACK):
+        pair_banks = [bank(b) for b in range(2)]
+
+        def look_up_first(i, j, tag):
+            first[i, j] = keep.tile([P, HALF], F32, name="first%d_%d" % (i, j), tag=tag, align_bytes=64)
+            look_up(0, i, j, first[i, j][:])
+
+        def turn_pair(j):
+            for b in range(2):
                 for i in range(2):
                     nc.tensor.matmul(
-                        pair[:, j, :], picked(s, i, j)[:, c0 : c0 + P], ident[:],
+                        pair_banks[b][:, j, :], first[i, j][:, b * P : (b + 1) * P], ident[:],
                         start=(i == 0), stop=(i == 1), is_transpose=True,
                     )
-            pair_turned = keep.tile(
-                [P, PACK, P], F32, name="pair_turned%d" % b, tag=("xt_raw1", "pair1", "pair2")[b]
-            )
+
+        def add_pair(b):
+            pair = pair_banks[b]
+            pair_turned = keep.tile([P, PACK, P], F32, name="pair_turned%d" % b, tag="pair_turned%d" % b, align_bytes=64)
             nc.scalar.copy(out=pair_turned[:], in_=pair[:])
             return pair_turned
 
-        def add_q(b, pair_turned):
-            total = bank((2, 3, 6)[b])
+        def add_q(b, terms):
+            total = bank(6 + b)
             for j in range(PACK):
-                for i, term in enumerate((q_turned[b], pair_turned)):
+                for i, term in enumerate(terms):
                     nc.tensor.matmul(
                         total[:, j, :], term[:, j, :], ident[:], start=(i == 0), stop=(i == 1), is_transpose=True
                     )
@@ -197,6 +197,12 @@ def tile_moe_buffer_read_twice_pl_kernel(
             nc.sync.dma_start(out=out_rows[:, :, b * P : (b + 1) * P], in_=y[:])
             return y
 
+        def q_back(b):
+            q = bank(2 + b)
+            for j in range(PACK):
+                nc.tensor.transpose(q[:, j, :], q_held[:, b, j, :], ident[:])
+            return q
+
         def quantise(t0, w, y_bf, tag):
             y_codes = keep.tile([P, w], U32, name="y_codes%d" % t0, tag=tag, align_bytes=64)
             nc.vector.quantize_mx(
@@ -204,40 +210,47 @@ def tile_moe_buffer_read_twice_pl_kernel(
             )
             nc.sync.dma_start(out=out_words[:, t0 : t0 + w], in_=y_codes[:].bitcast(I32))
 
-        for j in range(PACK):
-            for i in range(2):
-                look_up(0, i, j)
+        q_held = keep.tile([P, BLOCKS, PACK, P], F32, name="q_held", tag="xt_raw0")
+        for j, b in enumerate((2, 3, 0, 1)):
+            look_up_first(0, j, "first0_%d" % j)
+            look_up_first(1, j, "first1_0" if j == 0 else "chain%d" % (j - 1))
+            turn_pair(j)
+            quantise_xt(b, "xt_codes%d" % b)
+            q_turned(b)
         pairs = [add_pair(b) for b in range(2)]
-        ys = [add_q(b, pairs[b]) for b in range(2)]
-        for j in range(PACK):
-            for i in range(2):
-                look_up(1, i, j)
-        pair2 = add_pair(2)
-        q_last = bank(7)
-        for j in range(PACK):
-            nc.tensor.transpose(q_last[:, j, :], q_turned[BLOCKS - 1][:, j, :], ident[:])
-        y_bf_first = keep.tile([P, HALF, PACK], BF16, name="y_bf_first", tag="relay", align_bytes=64)
+        q2, q3 = q_back(2), q_back(3)
+        q_first = [q_held[:, b] for b in range(2)]
+        ys = [add_q(b, (q_first[b], pairs[b])) for b in range(2)]
+        y_bf_first = keep.tile([P, HALF, PACK], BF16, name="y_bf_first", align_bytes=64)
         for b in range(2):
             interleave(nc.scalar.copy, y_bf_first[:, b * P : (b + 1) * P, :], ys[b][:])
-        y2 = add_q(2, pair2)
-        y_bf2 = keep.tile([P, P, PACK], BF16, name="y_bf2", align_bytes=64)
-        interleave(nc.scalar.copy, y_bf2[:], y2[:])
 
+        second_a = keep.tile([P, PACK, HALF], F32, name="second_a", tag="chain3", align_bytes=64)
+        second_b = keep.tile([P, PACK, HALF], F32, name="second_b", tag="gate1_0", align_bytes=64)
         for j in range(PACK):
-            look_up(2, 0, j)
-        look_up(2, 1, 0)
-        part = keep.tile([P, PACK, P], F32, name="part", tag="part", align_bytes=64)
-        nc.vector.tensor_tensor(part[:], third[:, 0, :, :], q_last[:], ADD)
-        for j in range(1, PACK):
-            look_up(2, 1, j)
-        y3 = keep.tile([P, PACK, P], F32, name="y3")
-        nc.vector.tensor_tensor(y3[:], part[:], third[:, 1, :, :], ADD)
-        nc.sync.dma_start(out=out_rows[:, :, T - P :], in_=y3[:])
-        y_bf3 = keep.tile([P, P, PACK], BF16, name="y_bf3", align_bytes=64)
-        interleave(nc.vector.tensor_copy, y_bf3[:], y3[:])
-        quantise(0, HALF, y_bf_first, "part")
-        quantise(T - P, P, y_bf3, "codes3")
-        quantise(HALF, P, y_bf2, "gate0_1")
+            look_up(1, 0, j, second_a[:, j, :])
+        parts = []
+        for b, q in enumerate((q2, q3)):
+            look_up(1, 1, b, second_b[:, b, :])
+            part = keep.tile([P, PACK, P], F32, name="part%d" % b, tag="part%d" % b, align_bytes=64)
+            nc.vector.tensor_tensor(part[:], second_a[:, :, b * P : (b + 1) * P], q[:], ADD)
+            parts.append(part)
+        for j in range(2, PACK):
+            look_up(1, 1, j, second_b[:, j, :])
+        quantise(0, HALF, y_bf_first, "z_row2")
+        y_bf_last = []
+        for b, copy in enumerate((nc.scalar.copy, nc.vector.tensor_copy)):
+            y = keep.tile([P, PACK, P], F32, name="y%d" % (2 + b))
+            nc.vector.tensor_tensor(y[:], parts[b][:], second_b[:, :, b * P : (b + 1) * P], ADD)
+            nc.sync.dma_start(out=out_rows[:, :, HALF + b * P : HALF + (b + 1) * P], in_=y[:])
+            y_bf = keep.tile([P, P, PACK], BF16, name="y_bf%d" % (2 + b), align_bytes=64)
+            y_bf_last.append((copy, y_bf, y))
+        copy, y_bf, y = y_bf_last[0]
+        interleave(copy, y_bf[:], y[:])
+        quantise(HALF, P, y_bf, "codes2")
+        copy, y_bf, y = y_bf_last[1]
+        interleave(copy, y_bf[:], y[:])
+        quantise(HALF + P, P, y_bf, "codes3")
 
         for quad in range(4):
             queue = nc.sync if quad % 2 == 0 else nc.scalar

@@ -22,15 +22,25 @@ PACK = 4
 PASSES = K // (P * PACK)
 HALF = T // 2
 BLOCKS = T // P
-STRETCHES = ((0, HALF), (HALF, HALF))
+QUADRANTS = 4
+LINE = 4
+XT_ORDER = (2, 3, 0, 1)
 
 
-def load_scale_rows(queue, plane, scales):
-    for quad in range(4):
-        queue.dma_start(
-            out=plane[32 * quad : 32 * quad + 4, :, :].bitcast(I32),
+def scale_rows(quad):
+    return slice(32 * quad, 32 * quad + 4)
+
+
+def load_scale_rows(nc, plane, scales):
+    for quad in range(QUADRANTS):
+        nc.sync.dma_start(
+            out=plane[scale_rows(quad), :, :].bitcast(I32),
             in_=scales[:, 4 * quad : 4 * quad + 4, :].rearrange("z r c -> r z c").bitcast(I32),
         )
+
+
+def round_and_pack(copy, dst, src):
+    copy(out=dst.rearrange("p (c i) j -> p c j i", i=LINE), in_=src.rearrange("p j (c i) -> p c j i", i=LINE))
 
 
 def tile_moe_buffer_read_twice_pl_kernel(
@@ -55,7 +65,7 @@ def tile_moe_buffer_read_twice_pl_kernel(
         for plane in (wt_plane, wa_plane_raw):
             nc.vector.memset(plane[:].bitcast(I32), 0)
 
-        load_scale_rows(nc.sync, wa_rows, wa_scales)
+        load_scale_rows(nc, wa_rows, wa_scales)
         gate_cols = [keep.tile([P, PACK], F32, name="gate_col%d" % i) for i in range(2)]
         for col, gate in zip(gate_cols, (ga, gb)):
             nc.sync.dma_start(out=col[:], in_=gate.rearrange("o (p c) -> (o p) c", c=PACK))
@@ -63,7 +73,7 @@ def tile_moe_buffer_read_twice_pl_kernel(
         nc.sync.dma_start(out=wa_raw[:], in_=wa_words.rearrange("z p n r -> p z (n r)").bitcast(I32))
         xb_codes = keep.tile([P, PASSES, 2 * S], U8, name="xb_codes", align_bytes=64)
         nc.sync.dma_start(out=xb_codes[:].bitcast(I32), in_=xb_words.rearrange("z p c -> p z c").bitcast(I32))
-        load_scale_rows(nc.sync, xb_plane, xb_scales)
+        load_scale_rows(nc, xb_plane, xb_scales)
         offsets = [lists.tile([P, T // 16], U16, name="offsets%d" % i) for i in range(2)]
         nc.sync.dma_start(offsets[0][:], offs)
         nc.sync.dma_start(offsets[1][:], offs2)
@@ -72,11 +82,11 @@ def tile_moe_buffer_read_twice_pl_kernel(
         nc.sync.dma_start(out=xt_raw[1][:], in_=xt_rows[:, :, HALF:])
         wt_codes = keep.tile([P, 2 * N], U8, name="wt_codes", align_bytes=64)
         nc.sync.dma_start(out=wt_codes[:].bitcast(I32), in_=wt_words[0].bitcast(I32))
-        load_scale_rows(nc.sync, wt_plane, wt_scales)
+        load_scale_rows(nc, wt_plane, wt_scales)
         nc.sync.dma_start(out=xt_raw[0][:], in_=xt_rows[:, :, :HALF])
 
-        for quad in range(4):
-            rows = slice(32 * quad, 32 * quad + 4)
+        for quad in range(QUADRANTS):
+            rows = scale_rows(quad)
             nc.vector.tensor_copy(out=wa_plane_raw[rows, :, :].bitcast(I32), in_=wa_rows[rows, :, :].bitcast(I32))
         wa_planes = []
         for j in range(PACK):
@@ -86,8 +96,8 @@ def tile_moe_buffer_read_twice_pl_kernel(
         wa_codes = [keep.tile([P, N], U32, name="wa_codes%d" % z, align_bytes=64) for z in range(PASSES)]
         for z in range(PASSES):
             nc.vector.tensor_copy(
-                out=wa_codes[z][:].bitcast(I32).rearrange("p (j g i) -> p g j i", j=PACK, i=4),
-                in_=wa_raw[:, z, :].rearrange("p (g i j) -> p g j i", j=PACK, i=4),
+                out=wa_codes[z][:].bitcast(I32).rearrange("p (j g i) -> p g j i", j=PACK, i=LINE),
+                in_=wa_raw[:, z, :].rearrange("p (g i j) -> p g j i", j=PACK, i=LINE),
             )
 
         gates = []
@@ -95,17 +105,11 @@ def tile_moe_buffer_read_twice_pl_kernel(
             spread = bank(4 + i)
             for c in range(PACK):
                 nc.tensor.transpose(spread[:, c, :], gate_cols[i][:, c : c + 1].to_broadcast([P, P]), ident[:])
-            rows = []
-            for s, (t0, w) in enumerate(STRETCHES):
-                row = keep.tile([P, w], F32, name="gate%d_%d" % (i, s), tag="gate%d_%d" % (i, s), align_bytes=64)
-                nc.scalar.copy(
-                    out=row[:].rearrange("p (m c) -> p m c", c=PACK),
-                    in_=spread[:, :, t0 // PACK : (t0 + w) // PACK].rearrange("p c m -> p m c"),
-                )
-                rows.append(row)
-            gates.append(rows)
+            row = keep.tile([P, T], F32, name="gate_row%d" % i)
+            nc.scalar.copy(out=row[:].rearrange("p (m c) -> p m c", c=PACK), in_=spread[:].rearrange("p c m -> p m c"))
+            gates.append(row)
 
-        z_rows = []
+        z_slices = []
         for j in range(PACK):
             acc = bank(j)
             for z in range(PASSES):
@@ -118,143 +122,127 @@ def tile_moe_buffer_read_twice_pl_kernel(
                     start=(z == 0),
                     stop=(z == PASSES - 1),
                 )
-            z_row = keep.tile([P, S], F32, name="z_row%d" % j, tag="z_row%d" % j, align_bytes=64)
-            nc.scalar.copy(out=z_row[:], in_=acc[:].rearrange("p a b -> p (a b)"))
-            z_rows.append(z_row)
-
-        def interleave(copy, dst, src):
-            copy(out=dst.rearrange("p (c i) j -> p c j i", i=4), in_=src.rearrange("p j (c i) -> p c j i", i=4))
+            z_slice = keep.tile([P, S], F32, name="z_slice%d" % j, tag="z_slice%d" % j, align_bytes=64)
+            nc.scalar.copy(out=z_slice[:], in_=acc[:].rearrange("p a b -> p (a b)"))
+            z_slices.append(z_slice)
 
         xt_bf = {}
-        for j, b in enumerate((2, 3, 0, 1)):
+        for j, b in enumerate(XT_ORDER):
             xt_bf[b] = keep.tile([P, P, PACK], BF16, name="xt_bf%d" % b, tag="chain%d" % j, align_bytes=64)
-            interleave(nc.scalar.copy, xt_bf[b][:], xt_raw[b // 2][:, :, (b % 2) * P : (b % 2 + 1) * P])
+            round_and_pack(nc.scalar.copy, xt_bf[b][:], xt_raw[b // 2][:, :, (b % 2) * P : (b % 2 + 1) * P])
         xt_plane = keep.tile([P, T], U8, name="xt_plane", align_bytes=64)
-        xt_codes = {}
 
-        def quantise_xt(b, tag):
-            xt_codes[b] = keep.tile([P, P], U32, name="xt_codes%d" % b, tag=tag, align_bytes=64)
+        def q_turned(b):
+            xt_codes = keep.tile([P, P], U32, name="xt_codes%d" % b, align_bytes=64)
             nc.vector.quantize_mx(
-                out=xt_codes[b][:].bitcast(FP8X4),
+                out=xt_codes[:].bitcast(FP8X4),
                 scales=xt_plane[:, b * P : (b + 1) * P],
                 in_=xt_bf[b][:].rearrange("p t j -> p (t j)"),
             )
-
-        def q_turned(b):
-            flat = bank((2, 3, 6, 7)[b])[:].rearrange("p a b -> p (a b)")
+            acc = bank((2, 3, 6, 7)[b])[:].rearrange("p a b -> p (a b)")
             nc.tensor.matmul_mx(
-                out=flat,
-                lhsT=xt_codes[b][:].bitcast(FP8X4),
+                out=acc,
+                lhsT=xt_codes[:].bitcast(FP8X4),
                 lhsT_scale=xt_plane[:, b * P : (b + 1) * P],
                 rhs=wt_codes[:].bitcast(FP4X4),
                 rhs_scale=wt_plane[:, 0, :],
                 start=True,
                 stop=True,
             )
-            nc.scalar.copy(out=q_held[:, b], in_=flat.rearrange("p (m j) -> p j m", j=PACK))
+            return acc
 
-        first = {}
+        q_held = keep.tile([P, BLOCKS, PACK, P], F32, name="q_held", tag="xt_raw0")
 
-        def look_up(s, i, j, dst):
-            t0, w = STRETCHES[s]
-            nc.vector.tensor_tensor(
-                dst, z_rows[j][:].indirect(offsets[i][:, t0 // 16 : (t0 + w) // 16]), gates[i][s][:], MULT
-            )
+        def hold_q(b, acc):
+            nc.scalar.copy(out=q_held[:, b], in_=acc.rearrange("p (m j) -> p j m", j=PACK))
 
-        out_rows = out_0.rearrange("(p j) t -> p j t", j=PACK)
+        def look_up(h, i, j, dst):
+            entries = offsets[i][:, h * HALF // 16 : (h + 1) * HALF // 16]
+            nc.vector.tensor_tensor(dst, z_slices[j][:].indirect(entries), gates[i][:, h * HALF : (h + 1) * HALF], MULT)
+
+        def add_turned(dst, terms):
+            for i, term in enumerate(terms):
+                nc.tensor.matmul(dst, term, ident[:], start=(i == 0), stop=(i == len(terms) - 1), is_transpose=True)
+
+        out_slices = out_0.rearrange("(p j) t -> p j t", j=PACK)
         out_words = out_1[0].rearrange("p t r -> p (t r)").bitcast(I32)
         y_plane = keep.tile([P, T], U8, name="y_plane", align_bytes=64)
 
+        def hand_out_codes(h, y_bf, tag):
+            y_codes = keep.tile([P, HALF], U32, name="y_codes%d" % h, tag=tag, align_bytes=64)
+            nc.vector.quantize_mx(
+                out=y_codes[:].bitcast(FP8X4),
+                scales=y_plane[:, h * HALF : (h + 1) * HALF],
+                in_=y_bf[:].rearrange("p t j -> p (t j)"),
+            )
+            nc.sync.dma_start(out=out_words[:, h * HALF : (h + 1) * HALF], in_=y_codes[:].bitcast(I32))
+
         pair_banks = [bank(b) for b in range(2)]
-
-        def look_up_first(i, j, tag):
-            first[i, j] = keep.tile([P, HALF], F32, name="first%d_%d" % (i, j), tag=tag, align_bytes=64)
-            look_up(0, i, j, first[i, j][:])
-
-        def turn_pair(j):
+        q_banks = {}
+        for j, b_xt in enumerate(XT_ORDER):
+            tags = ("first0_%d" % j, "first1_0" if j == 0 else "chain%d" % (j - 1))
+            products = []
+            for i in range(2):
+                product = keep.tile([P, HALF], F32, name="first%d_%d" % (i, j), tag=tags[i], align_bytes=64)
+                look_up(0, i, j, product[:])
+                products.append(product)
             for b in range(2):
-                for i in range(2):
-                    nc.tensor.matmul(
-                        pair_banks[b][:, j, :], first[i, j][:, b * P : (b + 1) * P], ident[:],
-                        start=(i == 0), stop=(i == 1), is_transpose=True,
-                    )
+                add_turned(pair_banks[b][:, j, :], [product[:, b * P : (b + 1) * P] for product in products])
+            q_banks[b_xt] = q_turned(b_xt)
+        for b in XT_ORDER[:-1]:
+            hold_q(b, q_banks[b])
+        pairs = []
+        for b in range(2):
+            pair = keep.tile([P, PACK, P], F32, name="pair%d" % b, tag="pair%d" % b, align_bytes=64)
+            nc.scalar.copy(out=pair[:], in_=pair_banks[b][:])
+            pairs.append(pair)
+        hold_q(XT_ORDER[-1], q_banks[XT_ORDER[-1]])
 
-        def add_pair(b):
-            pair = pair_banks[b]
-            pair_turned = keep.tile([P, PACK, P], F32, name="pair_turned%d" % b, tag="pair_turned%d" % b, align_bytes=64)
-            nc.scalar.copy(out=pair_turned[:], in_=pair[:])
-            return pair_turned
-
-        def add_q(b, terms):
-            total = bank(6 + b)
-            for j in range(PACK):
-                for i, term in enumerate(terms):
-                    nc.tensor.matmul(
-                        total[:, j, :], term[:, j, :], ident[:], start=(i == 0), stop=(i == 1), is_transpose=True
-                    )
-            y = keep.tile([P, PACK, P], F32, name="y%d" % b)
-            nc.scalar.copy(out=y[:], in_=total[:])
-            nc.sync.dma_start(out=out_rows[:, :, b * P : (b + 1) * P], in_=y[:])
-            return y
-
-        def q_back(b):
+        q_last = []
+        for b in range(2, BLOCKS):
             q = bank(2 + b)
             for j in range(PACK):
                 nc.tensor.transpose(q[:, j, :], q_held[:, b, j, :], ident[:])
-            return q
+            q_last.append(q)
 
-        def quantise(t0, w, y_bf, tag):
-            y_codes = keep.tile([P, w], U32, name="y_codes%d" % t0, tag=tag, align_bytes=64)
-            nc.vector.quantize_mx(
-                out=y_codes[:].bitcast(FP8X4), scales=y_plane[:, t0 : t0 + w], in_=y_bf[:].rearrange("p t j -> p (t j)")
-            )
-            nc.sync.dma_start(out=out_words[:, t0 : t0 + w], in_=y_codes[:].bitcast(I32))
-
-        q_held = keep.tile([P, BLOCKS, PACK, P], F32, name="q_held", tag="xt_raw0")
-        for j, b in enumerate((2, 3, 0, 1)):
-            look_up_first(0, j, "first0_%d" % j)
-            look_up_first(1, j, "first1_0" if j == 0 else "chain%d" % (j - 1))
-            turn_pair(j)
-            quantise_xt(b, "xt_codes%d" % b)
-            q_turned(b)
-        pairs = [add_pair(b) for b in range(2)]
-        q2, q3 = q_back(2), q_back(3)
-        q_first = [q_held[:, b] for b in range(2)]
-        ys = [add_q(b, (q_first[b], pairs[b])) for b in range(2)]
+        y_first = []
+        for b in range(2):
+            total = bank(6 + b)
+            for j in range(PACK):
+                add_turned(total[:, j, :], (q_held[:, b, j, :], pairs[b][:, j, :]))
+            y = keep.tile([P, PACK, P], F32, name="y%d" % b)
+            nc.scalar.copy(out=y[:], in_=total[:])
+            nc.scalar.dma_start(out=out_slices[:, :, b * P : (b + 1) * P], in_=y[:])
+            y_first.append(y)
         y_bf_first = keep.tile([P, HALF, PACK], BF16, name="y_bf_first", align_bytes=64)
         for b in range(2):
-            interleave(nc.scalar.copy, y_bf_first[:, b * P : (b + 1) * P, :], ys[b][:])
+            round_and_pack(nc.scalar.copy, y_bf_first[:, b * P : (b + 1) * P, :], y_first[b][:])
 
-        second_a = keep.tile([P, PACK, HALF], F32, name="second_a", tag="chain3", align_bytes=64)
-        second_b = keep.tile([P, PACK, HALF], F32, name="second_b", tag="gate1_0", align_bytes=64)
+        second = keep.tile([P, 2, PACK, HALF], F32, name="second", tag="chain3", align_bytes=64)
         for j in range(PACK):
-            look_up(1, 0, j, second_a[:, j, :])
-        parts = []
-        for b, q in enumerate((q2, q3)):
-            look_up(1, 1, b, second_b[:, b, :])
-            part = keep.tile([P, PACK, P], F32, name="part%d" % b, tag="part%d" % b, align_bytes=64)
-            nc.vector.tensor_tensor(part[:], second_a[:, :, b * P : (b + 1) * P], q[:], ADD)
-            parts.append(part)
+            look_up(1, 0, j, second[:, 0, j, :])
+        part = keep.tile([P, PACK, HALF], F32, name="part")
+        for b, q in enumerate(q_last):
+            look_up(1, 1, b, second[:, 1, b, :])
+            cols = slice(b * P, (b + 1) * P)
+            nc.vector.tensor_tensor(part[:, :, cols], second[:, 0, :, cols], q[:], ADD)
+        y_last = keep.tile([P, PACK, HALF], F32, name="y_last")
+        look_up(1, 1, 2, second[:, 1, 2, :])
+        nc.vector.tensor_tensor(y_last[:, :2, :], part[:, :2, :], second[:, 1, :2, :], ADD)
+        nc.sync.dma_start(out=out_slices[:, :2, HALF:], in_=y_last[:, :2, :])
+        look_up(1, 1, 3, second[:, 1, 3, :])
         for j in range(2, PACK):
-            look_up(1, 1, j, second_b[:, j, :])
-        quantise(0, HALF, y_bf_first, "z_row2")
-        y_bf_last = []
-        for b, copy in enumerate((nc.scalar.copy, nc.vector.tensor_copy)):
-            y = keep.tile([P, PACK, P], F32, name="y%d" % (2 + b))
-            nc.vector.tensor_tensor(y[:], parts[b][:], second_b[:, :, b * P : (b + 1) * P], ADD)
-            nc.sync.dma_start(out=out_rows[:, :, HALF + b * P : HALF + (b + 1) * P], in_=y[:])
-            y_bf = keep.tile([P, P, PACK], BF16, name="y_bf%d" % (2 + b), align_bytes=64)
-            y_bf_last.append((copy, y_bf, y))
-        copy, y_bf, y = y_bf_last[0]
-        interleave(copy, y_bf[:], y[:])
-        quantise(HALF, P, y_bf, "codes2")
-        copy, y_bf, y = y_bf_last[1]
-        interleave(copy, y_bf[:], y[:])
-        quantise(HALF + P, P, y_bf, "codes3")
+            nc.vector.tensor_tensor(y_last[:, j, :], part[:, j, :], second[:, 1, j, :], ADD)
+        nc.sync.dma_start(out=out_slices[:, 2:, HALF:], in_=y_last[:, 2:, :])
 
-        for quad in range(4):
+        hand_out_codes(0, y_bf_first, "z_slice3")
+        y_bf_last = keep.tile([P, HALF, PACK], BF16, name="y_bf_last", tag="pair1", align_bytes=64)
+        for b, copy in enumerate((nc.scalar.copy, nc.vector.tensor_copy)):
+            round_and_pack(copy, y_bf_last[:, b * P : (b + 1) * P, :], y_last[:, :, b * P : (b + 1) * P])
+        hand_out_codes(1, y_bf_last, "y_codes1")
+
+        for quad in range(QUADRANTS):
             queue = nc.sync if quad % 2 == 0 else nc.scalar
             queue.dma_start(
-                out=out_2[0, 4 * quad : 4 * quad + 4, :].bitcast(I32),
-                in_=y_plane[32 * quad : 32 * quad + 4, :].bitcast(I32),
+                out=out_2[0, 4 * quad : 4 * quad + 4, :].bitcast(I32), in_=y_plane[scale_rows(quad), :].bitcast(I32)
             )

from contextlib import ExitStack

import concourse.mybir as mybir
from concourse.masks import make_identity

K, S, T, N, L = 1024, 512, 512, 512, 512
FLOPS = 2 * K * N * S + 2 * L * N * T

F32 = mybir.dt.float32
BF16 = mybir.dt.bfloat16
I32 = mybir.dt.int32
U32 = mybir.dt.uint32
U16 = mybir.dt.uint16
U8 = mybir.dt.uint8
FP8X4 = mybir.dt.float8_e4m3fn_x4
FP4X4 = mybir.dt.float4_e2m1fn_x4
MULT = mybir.AluOpType.mult
ADD = mybir.AluOpType.add

P = 128
PACK = 4
PASSES = K // (P * PACK)
HALF = T // 2
BLOCKS = T // P
QUADRANTS = 4
LINE = 4
XT_ORDER = (2, 3, 0, 1)


def scale_rows(quad):
    return slice(32 * quad, 32 * quad + 4)


def load_scale_rows(nc, plane, scales):
    for quad in range(QUADRANTS):
        nc.sync.dma_start(
            out=plane[scale_rows(quad), :, :].bitcast(I32),
            in_=scales[:, 4 * quad : 4 * quad + 4, :].rearrange("z r c -> r z c").bitcast(I32),
        )


def round_and_pack(copy, dst, src):
    copy(out=dst.rearrange("p (c i) j -> p c j i", i=LINE), in_=src.rearrange("p j (c i) -> p c j i", i=LINE))


def tile_moe_buffer_read_twice_pl_kernel(
    tc, xb_words, xb_scales, wa_words, wa_scales, ga, gb, xt, wt_words, wt_scales, offs, offs2, out_0, out_1, out_2
):
    nc = tc.nc
    with ExitStack() as ctx:
        lists = ctx.enter_context(tc.tile_pool(name="lists", bufs=1))
        keep = ctx.enter_context(tc.tile_pool(name="keep", bufs=1))
        psum = ctx.enter_context(tc.psum_pool(name="psum", bufs=1))

        def bank(b):
            return psum.tile([P, PACK, P], F32, name="bank%d" % b, tag="bank%d" % b)

        wa_rows = keep.tile([P, PASSES, N], U8, name="wa_rows", align_bytes=64)
        wa_plane_raw = keep.tile([P, PASSES, N], U8, name="wa_plane_raw", align_bytes=64)
        xb_plane = keep.tile([P, PASSES, S], U8, name="xb_plane", align_bytes=64)
        wt_plane = keep.tile([P, 1, N], U8, name="wt_plane", align_bytes=64)
        nc.gpsimd.memset(xb_plane[:].bitcast(I32), 0)
        ident = keep.tile([P, P], F32, name="ident")
        make_identity(nc, ident[:])
        for plane in (wt_plane, wa_plane_raw):
            nc.vector.memset(plane[:].bitcast(I32), 0)

        load_scale_rows(nc, wa_rows, wa_scales)
        gate_cols = [keep.tile([P, PACK], F32, name="gate_col%d" % i) for i in range(2)]
        for col, gate in zip(gate_cols, (ga, gb)):
            nc.sync.dma_start(out=col[:], in_=gate.rearrange("o (p c) -> (o p) c", c=PACK))
        wa_raw = keep.tile([P, PASSES, N], I32, name="wa_raw")
        nc.sync.dma_start(out=wa_raw[:], in_=wa_words.rearrange("z p n r -> p z (n r)").bitcast(I32))
        xb_codes = keep.tile([P, PASSES, 2 * S], U8, name="xb_codes", align_bytes=64)
        nc.sync.dma_start(out=xb_codes[:].bitcast(I32), in_=xb_words.rearrange("z p c -> p z c").bitcast(I32))
        load_scale_rows(nc, xb_plane, xb_scales)
        offsets = [lists.tile([P, T // 16], U16, name="offsets%d" % i) for i in range(2)]
        nc.sync.dma_start(offsets[0][:], offs)
        nc.sync.dma_start(offsets[1][:], offs2)
        xt_rows = xt.rearrange("(p j) t -> p j t", j=PACK)
        xt_raw = [keep.tile([P, PACK, HALF], F32, name="xt_raw%d" % h, tag="xt_raw%d" % h) for h in range(2)]
        nc.sync.dma_start(out=xt_raw[1][:], in_=xt_rows[:, :, HALF:])
        wt_codes = keep.tile([P, 2 * N], U8, name="wt_codes", align_bytes=64)
        nc.sync.dma_start(out=wt_codes[:].bitcast(I32), in_=wt_words[0].bitcast(I32))
        load_scale_rows(nc, wt_plane, wt_scales)
        nc.sync.dma_start(out=xt_raw[0][:], in_=xt_rows[:, :, :HALF])

        for quad in range(QUADRANTS):
            rows = scale_rows(quad)
            nc.vector.tensor_copy(out=wa_plane_raw[rows, :, :].bitcast(I32), in_=wa_rows[rows, :, :].bitcast(I32))
        wa_planes = []
        for j in range(PACK):
            plane = keep.tile([P, PASSES, P], U8, name="wa_plane%d" % j, tag="chain%d" % j, align_bytes=64)
            nc.vector.tensor_copy(out=plane[:], in_=wa_plane_raw[:].rearrange("p z (m j) -> p j z m", j=PACK)[:, j])
            wa_planes.append(plane)
        wa_codes = [keep.tile([P, N], U32, name="wa_codes%d" % z, align_bytes=64) for z in range(PASSES)]
        for z in range(PASSES):
            nc.vector.tensor_copy(
                out=wa_codes[z][:].bitcast(I32).rearrange("p (j g i) -> p g j i", j=PACK, i=LINE),
                in_=wa_raw[:, z, :].rearrange("p (g i j) -> p g j i", j=PACK, i=LINE),
            )

        gates = []
        for i in range(2):
            spread = bank(4 + i)
            for c in range(PACK):
                nc.tensor.transpose(spread[:, c, :], gate_cols[i][:, c : c + 1].to_broadcast([P, P]), ident[:])
            row = keep.tile([P, T], F32, name="gate_row%d" % i)
            nc.scalar.copy(out=row[:].rearrange("p (m c) -> p m c", c=PACK), in_=spread[:].rearrange("p c m -> p m c"))
            gates.append(row)

        z_slices = []
        for j in range(PACK):
            acc = bank(j)
            for z in range(PASSES):
                nc.tensor.matmul_mx(
                    out=acc[:].rearrange("p a b -> p (a b)"),
                    lhsT=wa_codes[z][:, j * P : (j + 1) * P].bitcast(FP8X4),
                    lhsT_scale=wa_planes[j][:, z, :],
                    rhs=xb_codes[:, z, :].bitcast(FP4X4),
                    rhs_scale=xb_plane[:, z, :],
                    start=(z == 0),
                    stop=(z == PASSES - 1),
                )
            z_slice = keep.tile([P, S], F32, name="z_slice%d" % j, tag="z_slice%d" % j, align_bytes=64)
            nc.scalar.copy(out=z_slice[:], in_=acc[:].rearrange("p a b -> p (a b)"))
            z_slices.append(z_slice)

        xt_bf = {}
        for j, b in enumerate(XT_ORDER):
            xt_bf[b] = keep.tile([P, P, PACK], BF16, name="xt_bf%d" % b, tag="chain%d" % j, align_bytes=64)
            round_and_pack(nc.scalar.copy, xt_bf[b][:], xt_raw[b // 2][:, :, (b % 2) * P : (b % 2 + 1) * P])
        xt_plane = keep.tile([P, T], U8, name="xt_plane", align_bytes=64)

        def q_turned(b):
            xt_codes = keep.tile([P, P], U32, name="xt_codes%d" % b, align_bytes=64)
            nc.vector.quantize_mx(
                out=xt_codes[:].bitcast(FP8X4),
                scales=xt_plane[:, b * P : (b + 1) * P],
                in_=xt_bf[b][:].rearrange("p t j -> p (t j)"),
            )
            acc = bank((2, 3, 6, 7)[b])[:].rearrange("p a b -> p (a b)")
            nc.tensor.matmul_mx(
                out=acc,
                lhsT=xt_codes[:].bitcast(FP8X4),
                lhsT_scale=xt_plane[:, b * P : (b + 1) * P],
                rhs=wt_codes[:].bitcast(FP4X4),
                rhs_scale=wt_plane[:, 0, :],
                start=True,
                stop=True,
            )
            return acc

        q_held = keep.tile([P, BLOCKS, PACK, P], F32, name="q_held", tag="xt_raw0")

        def hold_q(b, acc):
            nc.scalar.copy(out=q_held[:, b], in_=acc.rearrange("p (m j) -> p j m", j=PACK))

        def look_up(h, i, j, dst):
            entries = offsets[i][:, h * HALF // 16 : (h + 1) * HALF // 16]
            nc.vector.tensor_tensor(dst, z_slices[j][:].indirect(entries), gates[i][:, h * HALF : (h + 1) * HALF], MULT)

        def add_turned(dst, terms):
            for i, term in enumerate(terms):
                nc.tensor.matmul(dst, term, ident[:], start=(i == 0), stop=(i == len(terms) - 1), is_transpose=True)

        out_slices = out_0.rearrange("(p j) t -> p j t", j=PACK)
        out_words = out_1[0].rearrange("p t r -> p (t r)").bitcast(I32)
        y_plane = keep.tile([P, T], U8, name="y_plane", align_bytes=64)

        def hand_out_codes(h, y_bf, tag):
            y_codes = keep.tile([P, HALF], U32, name="y_codes%d" % h, tag=tag, align_bytes=64)
            nc.vector.quantize_mx(
                out=y_codes[:].bitcast(FP8X4),
                scales=y_plane[:, h * HALF : (h + 1) * HALF],
                in_=y_bf[:].rearrange("p t j -> p (t j)"),
            )
            nc.sync.dma_start(out=out_words[:, h * HALF : (h + 1) * HALF], in_=y_codes[:].bitcast(I32))

        pair_banks = [bank(b) for b in range(2)]
        q_banks = {}
        for j, b_xt in enumerate(XT_ORDER):
            tags = ("first0_%d" % j, "first1_0" if j == 0 else "chain%d" % (j - 1))
            products = []
            for i in range(2):
                product = keep.tile([P, HALF], F32, name="first%d_%d" % (i, j), tag=tags[i], align_bytes=64)
                look_up(0, i, j, product[:])
                products.append(product)
            for b in range(2):
                add_turned(pair_banks[b][:, j, :], [product[:, b * P : (b + 1) * P] for product in products])
            q_banks[b_xt] = q_turned(b_xt)
        for b in XT_ORDER[:-1]:
            hold_q(b, q_banks[b])
        pairs = []
        for b in range(2):
            pair = keep.tile([P, PACK, P], F32, name="pair%d" % b, tag="pair%d" % b, align_bytes=64)
            nc.scalar.copy(out=pair[:], in_=pair_banks[b][:])
            pairs.append(pair)
        hold_q(XT_ORDER[-1], q_banks[XT_ORDER[-1]])

        q_last = []
        for b in range(2, BLOCKS):
            q = bank(2 + b)
            for j in range(PACK):
                nc.tensor.transpose(q[:, j, :], q_held[:, b, j, :], ident[:])
            q_last.append(q)

        y_first = []
        for b in range(2):
            total = bank(6 + b)
            for j in range(PACK):
                add_turned(total[:, j, :], (q_held[:, b, j, :], pairs[b][:, j, :]))
            y = keep.tile([P, PACK, P], F32, name="y%d" % b)
            nc.scalar.copy(out=y[:], in_=total[:])
            nc.scalar.dma_start(out=out_slices[:, :, b * P : (b + 1) * P], in_=y[:])
            y_first.append(y)
        y_bf_first = keep.tile([P, HALF, PACK], BF16, name="y_bf_first", align_bytes=64)
        for b in range(2):
            round_and_pack(nc.scalar.copy, y_bf_first[:, b * P : (b + 1) * P, :], y_first[b][:])

        second = keep.tile([P, 2, PACK, HALF], F32, name="second", tag="chain3", align_bytes=64)
        for j in range(PACK):
            look_up(1, 0, j, second[:, 0, j, :])
        part = keep.tile([P, PACK, HALF], F32, name="part")
        for b, q in enumerate(q_last):
            look_up(1, 1, b, second[:, 1, b, :])
            cols = slice(b * P, (b + 1) * P)
            nc.vector.tensor_tensor(part[:, :, cols], second[:, 0, :, cols], q[:], ADD)
        y_last = keep.tile([P, PACK, HALF], F32, name="y_last")
        look_up(1, 1, 2, second[:, 1, 2, :])
        nc.vector.tensor_tensor(y_last[:, :2, :], part[:, :2, :], second[:, 1, :2, :], ADD)
        nc.sync.dma_start(out=out_slices[:, :2, HALF:], in_=y_last[:, :2, :])
        look_up(1, 1, 3, second[:, 1, 3, :])
        for j in range(2, PACK):
            nc.vector.tensor_tensor(y_last[:, j, :], part[:, j, :], second[:, 1, j, :], ADD)
        nc.sync.dma_start(out=out_slices[:, 2:, HALF:], in_=y_last[:, 2:, :])

        hand_out_codes(0, y_bf_first, "z_slice3")
        y_bf_last = keep.tile([P, HALF, PACK], BF16, name="y_bf_last", tag="pair1", align_bytes=64)
        for b, copy in enumerate((nc.scalar.copy, nc.vector.tensor_copy)):
            round_and_pack(copy, y_bf_last[:, b * P : (b + 1) * P, :], y_last[:, :, b * P : (b + 1) * P])
        hand_out_codes(1, y_bf_last, "y_codes1")

        for quad in range(QUADRANTS):
            queue = nc.sync if quad % 2 == 0 else nc.scalar
            queue.dma_start(
                out=out_2[0, 4 * quad : 4 * quad + 4, :].bitcast(I32), in_=y_plane[scale_rows(quad), :].bitcast(I32)
            )
